import numpy as np
import ml_dtypes


def mxq(x, axis, fmt="e4m3"):
    dtype, down = {"e4m3": (ml_dtypes.float8_e4m3fn, 7), "e5m2": (ml_dtypes.float8_e5m2, 14)}[fmt]
    v = np.moveaxis(np.asarray(x, np.float32).astype(ml_dtypes.bfloat16).astype(np.float64), axis, -1)
    blocks = v.reshape(v.shape[:-1] + (-1, 32))
    amax = np.abs(blocks).max(-1, keepdims=True)
    byte = np.maximum(np.where(amax > 0, np.frexp(amax)[1] - 1 + 127, 0) - down, 1)
    scale = np.exp2(byte - 127.0)
    codes = (blocks / scale).astype(np.float32).astype(dtype).astype(np.float64)
    return np.moveaxis((codes * scale).reshape(v.shape), -1, axis)


WIDE = False


def mx_kscale(k):
    if not WIDE:
        return np.ones(k)
    levels = np.array([10, -10, 5, -5, 0])
    if k % 512:
        return np.exp2(np.random.permutation(np.resize(levels, k // 32))).repeat(32)
    a = np.empty((k // 512, 16))
    for p in range(k // 512):
        a[p, :8] = np.random.permutation(np.resize(levels, 8))
        for g in range(8):
            far = levels[np.abs(levels - a[p, g]) >= 10]
            a[p, g + 8] = far[np.random.randint(len(far))]
    return np.exp2(a.ravel()).repeat(32)


def f64(x):
    return np.asarray(x).astype(np.float64)


def striped8(idx):
    return np.asarray(idx).reshape(8, -1, 16).transpose(0, 2, 1).reshape(128, -1).astype(np.uint16)


def unstriped8(offs):
    return offs.reshape(8, 16, -1).transpose(0, 2, 1).reshape(8, -1).astype(np.int64)


def pick8(x, idx, run):
    r = np.arange(len(x))
    return x[r[:, None], idx[r % (8 * run) // run]]


E2M1 = np.array([0.0, 0.5, 1.0, 1.5, 2.0, 3.0, 4.0, 6.0, -0.0, -0.5, -1.0, -1.5, -2.0, -3.0, -4.0, -6.0])


def pack_weight(w, fmt):
    k, n = w.shape
    w = f64(np.asarray(w, np.float32).astype(ml_dtypes.bfloat16)).reshape(k // 32, 32, n)
    amax = np.abs(w).max(1)
    if fmt == "e4m3":
        byte = np.frexp(amax)[1] - 1 + 127 - 7
    else:
        mant, ex = np.frexp(amax / 6.0)
        byte = np.where(mant > 0.5, ex, ex - 1) + 127
    byte = np.clip(np.where(amax > 0, byte, 1), 1, 254)
    scaled = (w * np.exp2(127.0 - byte)[:, None, :]).reshape(k, n).astype(np.float32)
    by_word = np.ascontiguousarray(scaled.reshape(k // 512, 128, 4, n).transpose(0, 1, 3, 2))
    if fmt == "e4m3":
        words = by_word.astype(ml_dtypes.float8_e4m3fn).view(np.uint8)
    else:
        c = by_word.astype(ml_dtypes.float4_e2m1fn).view(np.uint8) & 0xF
        words = (c[..., 0::2] | (c[..., 1::2] << 4)).reshape(k // 512, 128, 2 * n)
    return np.ascontiguousarray(words), np.ascontiguousarray(byte.astype(np.uint8).reshape(k // 512, 16, n))


def unpack_weight(words, scales, fmt):
    g, _, n = scales.shape
    words = np.ascontiguousarray(words).reshape(g, 128, n, -1)
    if fmt == "e4m3":
        vals = words.view(ml_dtypes.float8_e4m3fn).astype(np.float64)
    else:
        nib = np.empty((g, 128, n, 4), np.uint8)
        nib[..., 0::2] = words & 0xF
        nib[..., 1::2] = words >> 4
        vals = E2M1[nib]
    vals = vals * np.repeat(np.exp2(scales.astype(np.float64) - 127.0), 8, axis=1)[..., None]
    return vals.transpose(0, 1, 3, 2).reshape(g * 512, n)


D, T, I, Q = 512, 1024, 512, 128


def setup_inputs():
    n = np.random.standard_normal
    idx = np.stack([np.random.permutation(T)[:I] for _ in range(8)])
    idx2 = np.stack([np.random.permutation(T)[:I] for _ in range(8)])
    idx3 = np.stack([np.random.permutation(T)[:I] for _ in range(8)])
    fd = mx_kscale(D)
    keysp = pack_weight(n((D, T)) / fd[:, None], "e4m3")
    tagsp = pack_weight(n((D, T)) / fd[:, None], "e2m1")
    return {
        "query": (n((D, Q)) * 0.75 / np.sqrt(D) * fd[:, None]).astype(np.float32),
        "query2": (n((D, Q)) * 0.75 / np.sqrt(D) * fd[:, None]).astype(np.float32),
        "keys_words": keysp[0],
        "keys_scales": keysp[1],
        "tags_words": tagsp[0],
        "tags_scales": tagsp[1],
        "lam": (np.random.uniform(0.3, 0.7, (Q, 1))).astype(np.float32),
        "offs": striped8(idx),
        "offs2": striped8(idx2),
        "offs3": striped8(idx3),
    }


def reference(query, query2, keys_words, keys_scales, tags_words, tags_scales, lam, offs, offs2, offs3):
    idx = unstriped8(offs)
    idx2 = unstriped8(offs2)
    idx3 = unstriped8(offs3)
    keysu = unpack_weight(keys_words, keys_scales, "e4m3")
    tagsu = unpack_weight(tags_words, tags_scales, "e2m1")
    queryq = mxq(f64(query), 0, "e4m3")
    query2q = mxq(f64(query2), 0, "e4m3")
    a = queryq.T @ keysu + query2q.T @ tagsu
    f1 = np.zeros((Q, T))
    f1[np.arange(Q)[:, None], idx2[np.arange(Q) % 128 // 16]] = pick8(a, idx, 16)
    c1 = a + f1 * f64(lam)
    f2 = np.zeros((Q, T))
    f2[np.arange(Q)[:, None], idx2[np.arange(Q) % 128 // 16]] = pick8(c1, idx, 16)
    c2 = a + f2 * f64(lam)
    y = pick8(c2, idx3, 16)
    return y

@@ -1,0 +1,124 @@
+from contextlib import ExitStack
+
+import concourse.mybir as mybir
+
+D, T, I, Q = 512, 1024, 512, 128
+FLOPS = 2 * 2 * D * Q * T
+
+F32 = mybir.dt.float32
+BF16 = mybir.dt.bfloat16
+I32 = mybir.dt.int32
+U32 = mybir.dt.uint32
+U16 = mybir.dt.uint16
+U8 = mybir.dt.uint8
+FP8X4 = mybir.dt.float8_e4m3fn_x4
+FP4X4 = mybir.dt.float4_e2m1fn_x4
+COPY = mybir.ActivationFunctionType.Copy
+MULT = mybir.AluOpType.mult
+ADD = mybir.AluOpType.add
+
+P = 128
+PACK = 4
+HALF = I // 2
+TOKEN_RUNS = [(0, 512), (512, 768), (768, 1024)]
+
+
+def load_scale_plane(nc, plane, scales):
+    rows = scales[0].bitcast(I32).rearrange("(quad r) c -> r quad c", r=PACK)
+    words = plane[:].bitcast(I32)
+    for r in range(PACK):
+        nc.scalar.dma_start(out=words[r:P:32, :], in_=rows[r])
+
+
+def quantize_queries(nc, pool, raw, name):
+    woven = pool.tile([P, Q, PACK], BF16, name=name + "_woven", align_bytes=64)
+    codes = pool.tile([P, Q], U32, name=name + "_codes", align_bytes=64)
+    plane = pool.tile([P, Q], U8, name=name + "_plane", align_bytes=64)
+    nc.vector.tensor_copy(out=woven[:], in_=raw[:].rearrange("p j q -> p q j"))
+    nc.vector.quantize_mx(out=codes[:].bitcast(FP8X4), scales=plane[:], in_=woven[:].rearrange("p q j -> p (q j)"))
+    return codes, plane
+
+
+def gather_halves(nc, picked, table, offsets):
+    cols = HALF // 16
+    nc.vector.tensor_copy(picked[:, :HALF], table[:].indirect(offsets[:, :cols]))
+    nc.scalar.activation(picked[:, HALF:], table[:].indirect(offsets[:, cols:]), COPY)
+
+
+def tile_attend_samelinks_parts_kernel(
+    tc, query, query2, keys_words, keys_scales, tags_words, tags_scales, lam, offs, offs2, offs3, out
+):
+    nc = tc.nc
+    with ExitStack() as ctx:
+        pool = ctx.enter_context(tc.tile_pool(name="held", bufs=1))
+        psum = ctx.enter_context(tc.psum_pool(name="psum", bufs=1))
+
+        raw_q2 = pool.tile([P, PACK, Q], F32)
+        raw_q = pool.tile([P, PACK, Q], F32)
+        tag_words = pool.tile([P, 2 * T], U8, align_bytes=64)
+        key_words = pool.tile([P, T], U32, align_bytes=64)
+        tag_plane = pool.tile([P, T], U8, align_bytes=64)
+        key_plane = pool.tile([P, T], U8, align_bytes=64)
+        src_list = pool.tile([P, I // 16], U16)
+        dst_list = pool.tile([P, I // 16], U16)
+        out_list = pool.tile([P, I // 16], U16)
+        lam_col = pool.tile([P, 1], F32)
+
+        nc.sync.dma_start(out=raw_q2[:], in_=query2.rearrange("(p j) q -> p j q", j=PACK))
+        load_scale_plane(nc, tag_plane, tags_scales)
+        nc.sync.dma_start(out=tag_words[:].bitcast(I32), in_=tags_words[0].bitcast(I32))
+        nc.sync.dma_start(out=raw_q[:], in_=query.rearrange("(p j) q -> p j q", j=PACK))
+        nc.sync.dma_start(
+            out=key_words[:].bitcast(I32), in_=keys_words[0].rearrange("p t r -> p (t r)").bitcast(I32)
+        )
+        load_scale_plane(nc, key_plane, keys_scales)
+        nc.sync.dma_start(src_list[:], offs)
+        nc.sync.dma_start(dst_list[:], offs2)
+        nc.sync.dma_start(out_list[:], offs3)
+        nc.sync.dma_start(out=lam_col[:], in_=lam)
+
+        links = pool.tile([P, T], F32)
+        nc.gpsimd.memset(links[:], 0.0)
+
+        q2_codes, q2_plane = quantize_queries(nc, pool, raw_q2, "q2")
+        q_codes, q_plane = quantize_queries(nc, pool, raw_q, "q")
+
+        banks = [psum.tile([P, hi - lo], F32, name="bank%d" % lo) for lo, hi in TOKEN_RUNS]
+        for bank, (lo, hi) in zip(banks, TOKEN_RUNS):
+            nc.tensor.matmul_mx(
+                out=bank[:],
+                lhsT=q2_codes[:].bitcast(FP8X4),
+                lhsT_scale=q2_plane[:],
+                rhs=tag_words[:, 2 * lo : 2 * hi].bitcast(FP4X4),
+                rhs_scale=tag_plane[:, lo:hi],
+                start=True,
+                stop=False,
+            )
+        scores = pool.tile([P, T], F32)
+        for bank, (lo, hi) in zip(banks, TOKEN_RUNS):
+            nc.tensor.matmul_mx(
+                out=bank[:],
+                lhsT=q_codes[:].bitcast(FP8X4),
+                lhsT_scale=q_plane[:],
+                rhs=key_words[:, lo:hi].bitcast(FP8X4),
+                rhs_scale=key_plane[:, lo:hi],
+                start=False,
+                stop=True,
+            )
+            if lo == 0:
+                nc.scalar.copy(out=scores[:, lo:hi], in_=bank[:])
+            else:
+                nc.vector.tensor_copy(out=scores[:, lo:hi], in_=bank[:])
+
+        sums = scores
+        for hop in range(2):
+            picked = pool.tile([P, I], F32, name="picked%d" % hop)
+            gather_halves(nc, picked, sums, src_list)
+            nc.vector.tensor_copy(links[:].indirect(dst_list[:]), picked[:])
+            sums = pool.tile([P, T], F32, name="sums%d" % hop)
+            nc.vector.scalar_tensor_tensor(sums[:], links[:], lam_col[:], scores[:], MULT, ADD)
+
+        result = pool.tile([P, I], F32)
+        gather_halves(nc, result, sums, out_list)
+        nc.sync.dma_start(out=out[:, :HALF], in_=result[:, :HALF])
+        nc.scalar.dma_start(out=out[:, HALF:], in_=result[:, HALF:])

@@ -20,14 +20,14 @@ ADD = mybir.AluOpType.add
 P = 128
 PACK = 4
 HALF = I // 2
-TOKEN_RUNS = [(0, 512), (512, 768), (768, 1024)]
+TOKEN_RUNS = [(0, 256), (256, 512), (512, 768), (768, 896), (896, 1024)]
 
 
 def load_scale_plane(nc, plane, scales):
     rows = scales[0].bitcast(I32).rearrange("(quad r) c -> r quad c", r=PACK)
     words = plane[:].bitcast(I32)
     for r in range(PACK):
-        nc.scalar.dma_start(out=words[r:P:32, :], in_=rows[r])
+        nc.sync.dma_start(out=words[r:P:32, :], in_=rows[r])
 
 
 def quantize_queries(nc, pool, raw, name):
@@ -95,7 +95,7 @@ def tile_attend_samelinks_parts_kernel(
                 stop=False,
             )
         scores = pool.tile([P, T], F32)
-        for bank, (lo, hi) in zip(banks, TOKEN_RUNS):
+        for n, (bank, (lo, hi)) in enumerate(zip(banks, TOKEN_RUNS)):
             nc.tensor.matmul_mx(
                 out=bank[:],
                 lhsT=q_codes[:].bitcast(FP8X4),
@@ -105,7 +105,7 @@ def tile_attend_samelinks_parts_kernel(
                 start=False,
                 stop=True,
             )
-            if lo == 0:
+            if n % 2 == 0:
                 nc.scalar.copy(out=scores[:, lo:hi], in_=bank[:])
             else:
                 nc.vector.tensor_copy(out=scores[:, lo:hi], in_=bank[:])

@@ -20,7 +20,8 @@ ADD = mybir.AluOpType.add
 P = 128
 PACK = 4
 HALF = I // 2
-TOKEN_RUNS = [(0, 256), (256, 512), (512, 768), (768, 896), (896, 1024)]
+SPLIT = 688
+TOKEN_RUNS = [(0, 512), (512, 768), (768, 896), (896, 1024)]
 
 
 def load_scale_plane(nc, plane, scales):
@@ -68,17 +69,19 @@ def tile_attend_samelinks_parts_kernel(
         load_scale_plane(nc, tag_plane, tags_scales)
         nc.sync.dma_start(out=tag_words[:].bitcast(I32), in_=tags_words[0].bitcast(I32))
         nc.sync.dma_start(out=raw_q[:], in_=query.rearrange("(p j) q -> p j q", j=PACK))
-        nc.sync.dma_start(
-            out=key_words[:].bitcast(I32), in_=keys_words[0].rearrange("p t r -> p (t r)").bitcast(I32)
-        )
+        keys_hbm = keys_words[0].rearrange("p t r -> p (t r)").bitcast(I32)
+        nc.sync.dma_start(out=key_words[:, : T // 2].bitcast(I32), in_=keys_hbm[:, : T // 2])
         load_scale_plane(nc, key_plane, keys_scales)
+        nc.sync.dma_start(out=key_words[:, T // 2 :].bitcast(I32), in_=keys_hbm[:, T // 2 :])
         nc.sync.dma_start(src_list[:], offs)
         nc.sync.dma_start(dst_list[:], offs2)
         nc.sync.dma_start(out_list[:], offs3)
-        nc.sync.dma_start(out=lam_col[:], in_=lam)
+        nc.gpsimd.dma_start(out=lam_col[:], in_=lam)
+        lam_row = pool.tile([P, I], F32)
+        nc.scalar.copy(out=lam_row[:], in_=lam_col[:].to_broadcast([P, I]))
 
         links = pool.tile([P, T], F32)
-        nc.gpsimd.memset(links[:], 0.0)
+        nc.vector.memset(links[:], 0.0)
 
         q2_codes, q2_plane = quantize_queries(nc, pool, raw_q2, "q2")
         q_codes, q_plane = quantize_queries(nc, pool, raw_q, "q")
@@ -114,9 +117,13 @@ def tile_attend_samelinks_parts_kernel(
         for hop in range(2):
             picked = pool.tile([P, I], F32, name="picked%d" % hop)
             gather_halves(nc, picked, sums, src_list)
-            nc.vector.tensor_copy(links[:].indirect(dst_list[:]), picked[:])
+            nc.vector.tensor_tensor(links[:].indirect(dst_list[:]), picked[:], lam_row[:], MULT)
             sums = pool.tile([P, T], F32, name="sums%d" % hop)
-            nc.vector.scalar_tensor_tensor(sums[:], links[:], lam_col[:], scores[:], MULT, ADD)
+            nc.gpsimd.tensor_tensor(sums[:, SPLIT:], links[:, SPLIT:], scores[:, SPLIT:], ADD)
+            for bank, (lo, hi) in zip(banks, TOKEN_RUNS):
+                end = min(hi, SPLIT)
+                if end > lo:
+                    nc.vector.tensor_tensor(sums[:, lo:end], links[:, lo:end], bank[:, : end - lo], ADD)
 
         result = pool.tile([P, I], F32)
         gather_halves(nc, result, sums, out_list)

from contextlib import ExitStack

import concourse.mybir as mybir

D, T, I, Q = 512, 1024, 512, 128
FLOPS = 2 * 2 * D * Q * T

F32 = mybir.dt.float32
BF16 = mybir.dt.bfloat16
I32 = mybir.dt.int32
U32 = mybir.dt.uint32
U16 = mybir.dt.uint16
U8 = mybir.dt.uint8
FP8X4 = mybir.dt.float8_e4m3fn_x4
FP4X4 = mybir.dt.float4_e2m1fn_x4
COPY = mybir.ActivationFunctionType.Copy
MULT = mybir.AluOpType.mult
ADD = mybir.AluOpType.add

P = 128
PACK = 4
HALF = I // 2
SPLIT = 688
TOKEN_RUNS = [(0, 512), (512, 768), (768, 896), (896, 1024)]


def load_scale_plane(nc, plane, scales):
    rows = scales[0].bitcast(I32).rearrange("(quad r) c -> r quad c", r=PACK)
    words = plane[:].bitcast(I32)
    for r in range(PACK):
        nc.sync.dma_start(out=words[r:P:32, :], in_=rows[r])


def quantize_queries(nc, pool, raw, name):
    woven = pool.tile([P, Q, PACK], BF16, name=name + "_woven", align_bytes=64)
    codes = pool.tile([P, Q], U32, name=name + "_codes", align_bytes=64)
    plane = pool.tile([P, Q], U8, name=name + "_plane", align_bytes=64)
    nc.vector.tensor_copy(out=woven[:], in_=raw[:].rearrange("p j q -> p q j"))
    nc.vector.quantize_mx(out=codes[:].bitcast(FP8X4), scales=plane[:], in_=woven[:].rearrange("p q j -> p (q j)"))
    return codes, plane


def gather_halves(nc, picked, table, offsets):
    cols = HALF // 16
    nc.vector.tensor_copy(picked[:, :HALF], table[:].indirect(offsets[:, :cols]))
    nc.scalar.activation(picked[:, HALF:], table[:].indirect(offsets[:, cols:]), COPY)


def tile_attend_samelinks_parts_kernel(
    tc, query, query2, keys_words, keys_scales, tags_words, tags_scales, lam, offs, offs2, offs3, out
):
    nc = tc.nc
    with ExitStack() as ctx:
        pool = ctx.enter_context(tc.tile_pool(name="held", bufs=1))
        psum = ctx.enter_context(tc.psum_pool(name="psum", bufs=1))

        raw_q2 = pool.tile([P, PACK, Q], F32)
        raw_q = pool.tile([P, PACK, Q], F32)
        tag_words = pool.tile([P, 2 * T], U8, align_bytes=64)
        key_words = pool.tile([P, T], U32, align_bytes=64)
        tag_plane = pool.tile([P, T], U8, align_bytes=64)
        key_plane = pool.tile([P, T], U8, align_bytes=64)
        src_list = pool.tile([P, I // 16], U16)
        dst_list = pool.tile([P, I // 16], U16)
        out_list = pool.tile([P, I // 16], U16)
        lam_col = pool.tile([P, 1], F32)

        nc.sync.dma_start(out=raw_q2[:], in_=query2.rearrange("(p j) q -> p j q", j=PACK))
        load_scale_plane(nc, tag_plane, tags_scales)
        nc.sync.dma_start(out=tag_words[:].bitcast(I32), in_=tags_words[0].bitcast(I32))
        nc.sync.dma_start(out=raw_q[:], in_=query.rearrange("(p j) q -> p j q", j=PACK))
        keys_hbm = keys_words[0].rearrange("p t r -> p (t r)").bitcast(I32)
        nc.sync.dma_start(out=key_words[:, : T // 2].bitcast(I32), in_=keys_hbm[:, : T // 2])
        load_scale_plane(nc, key_plane, keys_scales)
        nc.sync.dma_start(out=key_words[:, T // 2 :].bitcast(I32), in_=keys_hbm[:, T // 2 :])
        nc.sync.dma_start(src_list[:], offs)
        nc.sync.dma_start(dst_list[:], offs2)
        nc.sync.dma_start(out_list[:], offs3)
        nc.gpsimd.dma_start(out=lam_col[:], in_=lam)
        lam_row = pool.tile([P, I], F32)
        nc.scalar.copy(out=lam_row[:], in_=lam_col[:].to_broadcast([P, I]))

        links = pool.tile([P, T], F32)
        nc.vector.memset(links[:], 0.0)

        q2_codes, q2_plane = quantize_queries(nc, pool, raw_q2, "q2")
        q_codes, q_plane = quantize_queries(nc, pool, raw_q, "q")

        banks = [psum.tile([P, hi - lo], F32, name="bank%d" % lo) for lo, hi in TOKEN_RUNS]
        for bank, (lo, hi) in zip(banks, TOKEN_RUNS):
            nc.tensor.matmul_mx(
                out=bank[:],
                lhsT=q2_codes[:].bitcast(FP8X4),
                lhsT_scale=q2_plane[:],
                rhs=tag_words[:, 2 * lo : 2 * hi].bitcast(FP4X4),
                rhs_scale=tag_plane[:, lo:hi],
                start=True,
                stop=False,
            )
        scores = pool.tile([P, T], F32)
        for n, (bank, (lo, hi)) in enumerate(zip(banks, TOKEN_RUNS)):
            nc.tensor.matmul_mx(
                out=bank[:],
                lhsT=q_codes[:].bitcast(FP8X4),
                lhsT_scale=q_plane[:],
                rhs=key_words[:, lo:hi].bitcast(FP8X4),
                rhs_scale=key_plane[:, lo:hi],
                start=False,
                stop=True,
            )
            if n % 2 == 0:
                nc.scalar.copy(out=scores[:, lo:hi], in_=bank[:])
            else:
                nc.vector.tensor_copy(out=scores[:, lo:hi], in_=bank[:])

        sums = scores
        for hop in range(2):
            picked = pool.tile([P, I], F32, name="picked%d" % hop)
            gather_halves(nc, picked, sums, src_list)
            nc.vector.tensor_tensor(links[:].indirect(dst_list[:]), picked[:], lam_row[:], MULT)
            sums = pool.tile([P, T], F32, name="sums%d" % hop)
            nc.gpsimd.tensor_tensor(sums[:, SPLIT:], links[:, SPLIT:], scores[:, SPLIT:], ADD)
            for bank, (lo, hi) in zip(banks, TOKEN_RUNS):
                end = min(hi, SPLIT)
                if end > lo:
                    nc.vector.tensor_tensor(sums[:, lo:end], links[:, lo:end], bank[:, : end - lo], ADD)

        result = pool.tile([P, I], F32)
        gather_halves(nc, result, sums, out_list)
        nc.sync.dma_start(out=out[:, :HALF], in_=result[:, :HALF])
        nc.scalar.dma_start(out=out[:, HALF:], in_=result[:, HALF:])
